import numpy as np
CORES = [66,70,74,78,82,86,90,94,98,102,106,110,114,118,122,126]
N = 16
T = 64
def entries(a): return a.T.reshape(-1)
def pack(v, P): return np.ascontiguousarray(np.asarray(v, np.int32).reshape(-1, P).T)
def lists(rng, how):
    Q = rng.permutation(N * T)
    if how == "stay": Q = np.arange(N * T)
    if how == "own": Q = np.concatenate([T * r + rng.permutation(T) for r in range(N)])
    if how == "shift": Q = (np.arange(N * T) + T * int(rng.integers(1, N)) + 1) % (N * T)
    if how == "deal": Q = (np.arange(N * T) % N) * T + np.arange(N * T) // N
    if how == "block": s = int(rng.integers(1, N)); Q = np.concatenate([T * ((r + s) % N) + rng.permutation(T) for r in range(N)])
    return {"goes": np.broadcast_to(pack(Q, 16), (N, 16, N * T // 16)).copy()}
def setup_inputs(rng):
    return dict({"x": rng.standard_normal((N, 128, T), dtype=np.float32)}, **lists(rng, "uniform"))
def setup_inputs_block(rng):
    d = setup_inputs(rng); d.update(lists(rng, "block"))
    for k in ("x",): d[k] = (d[k].astype(np.float32) * 1048576.0).astype(d[k].dtype)
    return d
def setup_inputs_deal(rng):
    d = setup_inputs(rng); d.update(lists(rng, "deal"))
    for k in ("x",): d[k] = (d[k].astype(np.float32) * (1 / 1024.0)).astype(d[k].dtype)
    return d
def setup_inputs_own(rng):
    d = setup_inputs(rng); d.update(lists(rng, "own"))
    return d
def setup_inputs_shift(rng):
    d = setup_inputs(rng); d.update(lists(rng, "shift"))
    return d
def setup_inputs_stay(rng):
    d = setup_inputs(rng); d.update(lists(rng, "stay"))
    return d
def check_inputs(x):
    bad = []
    if x["goes"].min() < 0 or x["goes"].max() >= N * T: bad.append("goes out of range")
    if not np.array_equal(np.sort(entries(x["goes"][0])), np.arange(N * T)): bad.append("goes isn't a permutation")
    if not all(np.array_equal(a, x["goes"][0]) for a in x["goes"]): bad.append("goes isn't alike on all ranks")
    return bad
def reference(x, goes):
    A = np.concatenate(list(x), axis=1); Y = np.zeros_like(A)
    Y[:, entries(goes[0])] = A
    return {"y": np.stack([Y[:, T * r:T * r + T] for r in range(N)])}

@@ -1,0 +1,140 @@
+from concourse.bass import DstId, RemoteDMATransfer
+from concourse.mybir import AluOpType, AxisListType, ActivationFunctionType
+
+N = 16
+C = 64
+R = 8
+NC = N * C
+
+SCRATCH = {
+    "xs": ("dram", [N, 128, 4], "float32"),
+    "mid": ("dram", [N, 128, 4], "float32"),
+    "snd": ("dram", [N, 128, 4], "float32"),
+    "ybuf": ("dram", [N, 128, 4], "float32"),
+    "wdat": ("sbuf", [128, NC], "float32"),
+    "ydat": ("sbuf", [128, NC], "float32"),
+    "win": ("sbuf", [128, NC], "float32"),
+    "vals": ("sbuf", [128, 128], "float32"),
+    "ones": ("sbuf", [128, 128], "float32"),
+    "ident": ("sbuf", [128, 128], "float32"),
+    "lead": ("sbuf", [128, 8], "float32"),
+    "sel": ("sbuf", [128, 1], "float32"),
+    "g8i": ("sbuf", [128, 8], "int32"),
+    "g8u": ("sbuf", [128, 8], "uint16"),
+    "invp": ("sbuf", [128, 8], "float32"),
+    "off": ("sbuf", [128, C], "uint16"),
+    "ps1": ("psum", [128, 512], "float32"),
+    "ps2": ("psum", [128, 512], "float32"),
+}
+SEMAPHORES = ["m_ones", "m_win", "m_off", "m_w", "io_v", "io_i", "io_e", "selr", "gl", "cvt", "scat", "mm1", "cp1",
+              "mm2", "offr", "xl", "own1", "arr1", "ld2", "gv", "gs", "st2", "own2", "arr2", "sent", "fin"]
+
+
+def _engines(mask):
+    return [e for e in range(mask.bit_length()) if (mask >> e) & 1]
+
+
+def _hops(topo, a, b):
+    ca, cb = topo.chip(a), topo.chip(b)
+    if ca == cb:
+        return 0
+    if topo.mates(ca, cb) or topo.same_plane(ca, cb):
+        return 1
+    return 2
+
+
+def _all_to_all(g, core, T, topo, src, dst, remote_sem, local_sem):
+    me = T.rank_of(core)
+    peers = sorted([c for c in T.cores if c != core], key=lambda c: -_hops(topo, core, c))
+    width = min(len(_engines(topo.mask(core, c))) for c in peers)
+    n = 0
+    for i in range(0, len(peers), width):
+        used, trs = [], []
+        for c in peers[i:i + width]:
+            e = [k for k in _engines(topo.mask(core, c)) if k not in used][0]
+            used.append(e)
+            rid, pid, _ = topo.addr(c)
+            trs.append(RemoteDMATransfer(dst_ids=[DstId(rid=rid, pnc=pid)], dma_engine_mask=1 << e,
+                                         remote_sem=remote_sem, src=src[T.rank_of(c)], dst=dst[me]))
+            n += 1
+        g.remote_dma_fused(trs, local_sem=local_sem)
+    return n
+
+
+def rank_program(g, core, T, topo):
+    r = T.rank_of(core)
+    if r is None:
+        return
+    S = T.sem
+    v, sc, sy, te = g.vector, g.scalar, g.sync, g.tensor
+
+    sy.dma_start(T.xs[:], T.x[:]).then_inc(S.xl, 16)
+    sy.dma_start(T.mid[r], T.x[R * r:R * r + R, :]).then_inc(S.own1, 16)
+    for k in range(8):
+        sc.dma_start(T.g8i[16 * k:16 * k + 16, :], T.goes[:, 8 * k:8 * k + 8]).then_inc(S.gl, 16)
+
+    v.memset(T.ones[:], 1.0).then_inc(S.m_ones, 1)
+    v.memset(T.win[:], 0.0).then_inc(S.m_win, 1)
+    v.memset(T.off[:], 0).then_inc(S.m_off, 1)
+    v.memset(T.wdat[:], 0.0).then_inc(S.m_w, 1)
+    g.iota(T.vals[:], [[1, 128]], 0, 8, allow_small_or_imprecise_dtypes=True).then_inc(S.io_v, 1)
+    g.wait_ge(S.m_ones, 1)
+    g.affine_select(T.lead[:], T.ones[:, 0:8], [[-16, 8]], AluOpType.is_equal, 0.0, 0, 1).then_inc(S.io_e, 1)
+    g.affine_select(T.ident[:], T.ones[:], [[-1, 128]], AluOpType.is_equal, 0.0, 0, 1).then_inc(S.io_i, 1)
+
+    g.wait_ge(S.xl, 16)
+    sent = _all_to_all(g, core, T, topo, T.xs, T.mid, S.arr1, S.sent)
+
+    v.wait_ge(S.io_e, 1)
+    v.tensor_reduce(T.sel[:, 0:1], T.lead[:, 0:8], AxisListType.X, AluOpType.add).then_inc(S.selr, 1)
+    v.wait_ge(S.gl, 16 * 8)
+    v.tensor_copy(T.g8u[:], T.g8i[:]).then_inc(S.cvt, 1)
+    v.wait_ge(S.cvt, 1)
+    v.wait_ge(S.io_v, 1)
+    v.wait_ge(S.m_win, 1)
+    v.tensor_copy(T.win[:, 0:NC].indirect(T.g8u[:, 0:8]), T.vals[:, 0:128]).then_inc(S.scat, 1)
+    te.wait_ge(S.scat, 1)
+    te.wait_ge(S.selr, 1)
+    for k in range(8):
+        te.matmul(T.ps1[:, k:k + 1], T.win[:, 128 * k:128 * k + 128], T.sel[:, 0:1], True, True).then_inc(S.mm1, 1)
+    v.wait_ge(S.mm1, 8)
+    v.tensor_copy(T.invp[:], T.ps1[:, 0:8]).then_inc(S.cp1, 1)
+    te.wait_ge(S.cp1, 1)
+    te.wait_ge(S.io_i, 1)
+    for a in range(8):
+        te.matmul(T.ps2[0:16, a:C:8], T.ident[:, 16 * a:16 * a + 16], T.invp[:, 0:8], True, True).then_inc(S.mm2, 1)
+    v.wait_ge(S.mm2, 8)
+    v.wait_ge(S.m_off, 1)
+    v.tensor_copy(T.off[0:16, :], T.ps2[0:16, 0:C]).then_inc(S.offr, 1)
+
+    for q_, qs in ((sy, range(0, R, 2)), (sc, range(1, R, 2))):
+        q_.wait_ge(S.arr1, N - 1)
+        q_.wait_ge(S.own1, 16)
+        q_.wait_ge(S.m_w, 1)
+        for q in qs:
+            q_.dma_start(T.wdat[q:q + 1, :], T.mid[:, 16 * q:16 * q + 16, :]).then_inc(S.ld2, 16)
+
+    h = NC // 2
+    v.wait_ge(S.offr, 1)
+    v.wait_ge(S.ld2, 16 * R)
+    v.tensor_copy(T.ydat[:, 0:h], T.wdat[:, 0:NC].indirect(T.off[:, 0:C // 2])).then_inc(S.gv, 1)
+    sc.wait_ge(S.offr, 1)
+    sc.wait_ge(S.ld2, 16 * R)
+    sc.activation(T.ydat[:, h:NC], T.wdat[:, 0:NC].indirect(T.off[:, C // 2:C]),
+                  ActivationFunctionType.Copy).then_inc(S.gs, 1)
+
+    for q_, qs in ((sy, range(0, R, 2)), (sc, range(1, R, 2))):
+        q_.wait_ge(S.gv, 1)
+        q_.wait_ge(S.gs, 1)
+        for q in qs:
+            q_.dma_start(T.snd[:, 16 * q:16 * q + 16, :], T.ydat[q:q + 1, :]).then_inc(S.st2, 16)
+    sy.dma_start(T.ybuf[r], T.ydat[0:R, C * r:C * r + C]).then_inc(S.own2, 16)
+
+    g.wait_ge(S.st2, 16 * R)
+    sent += _all_to_all(g, core, T, topo, T.snd, T.ybuf, S.arr2, S.sent)
+
+    sy.wait_ge(S.arr2, N - 1)
+    sy.wait_ge(S.own2, 16)
+    sy.dma_start(T.y[:], T.ybuf[:]).then_inc(S.fin, 16)
+    sy.wait_ge(S.fin, 16)
+    g.wait_ge(S.sent, sent)

@@ -3,62 +3,51 @@ from concourse.mybir import AluOpType, AxisListType, ActivationFunctionType
 
 N = 16
 C = 64
-R = 8
 NC = N * C
 
 SCRATCH = {
-    "xs": ("dram", [N, 128, 4], "float32"),
-    "mid": ("dram", [N, 128, 4], "float32"),
-    "snd": ("dram", [N, 128, 4], "float32"),
-    "ybuf": ("dram", [N, 128, 4], "float32"),
-    "wdat": ("sbuf", [128, NC], "float32"),
-    "ydat": ("sbuf", [128, NC], "float32"),
-    "win": ("sbuf", [128, NC], "float32"),
-    "vals": ("sbuf", [128, 128], "float32"),
-    "ones": ("sbuf", [128, 128], "float32"),
-    "ident": ("sbuf", [128, 128], "float32"),
-    "lead": ("sbuf", [128, 8], "float32"),
-    "sel": ("sbuf", [128, 1], "float32"),
+    "xg": ("sbuf", [128, 256], "float32"),
+    "sm": ("sbuf", [128, 256], "float32"),
+    "z": ("sbuf", [128, 256], "float32"),
+    "yo": ("sbuf", [128, C], "float32"),
+    "win": ("sbuf", [128, NC], "bfloat16"),
+    "vals": ("sbuf", [128, 128], "bfloat16"),
+    "jm1": ("sbuf", [128, 128], "float32"),
+    "gw": ("sbuf", [128, 8], "float32"),
+    "one8": ("sbuf", [128, 8], "float32"),
+    "ones": ("sbuf", [128, 512], "float32"),
+    "comb": ("sbuf", [128, 16], "float32"),
+    "sel0": ("sbuf", [128, 1], "float32"),
+    "rhsf": ("sbuf", [128, 1], "float32"),
+    "rhsb": ("sbuf", [128, 1], "bfloat16"),
+    "rep": ("sbuf", [128, 512], "float32"),
     "g8i": ("sbuf", [128, 8], "int32"),
     "g8u": ("sbuf", [128, 8], "uint16"),
     "invp": ("sbuf", [128, 8], "float32"),
-    "off": ("sbuf", [128, C], "uint16"),
+    "t1": ("sbuf", [128, 16], "float32"),
+    "l2": ("sbuf", [128, 16], "uint16"),
+    "ii": ("sbuf", [128, 4], "int32"),
+    "pa": ("sbuf", [128, 4], "int32"),
+    "j1": ("sbuf", [128, 4], "int32"),
+    "j2": ("sbuf", [128, 4], "int32"),
+    "jj": ("sbuf", [128, 4], "int32"),
+    "p64": ("sbuf", [128, 4], "int32"),
+    "lfi": ("sbuf", [128, 4], "int32"),
+    "lf": ("sbuf", [128, 4], "uint16"),
     "ps1": ("psum", [128, 512], "float32"),
     "ps2": ("psum", [128, 512], "float32"),
 }
-SEMAPHORES = ["m_ones", "m_win", "m_off", "m_w", "io_v", "io_i", "io_e", "selr", "gl", "cvt", "scat", "mm1", "cp1",
-              "mm2", "offr", "xl", "own1", "arr1", "ld2", "gv", "gs", "st2", "own2", "arr2", "sent", "fin"]
+SEMAPHORES = ["xl", "gl", "m_o8", "m_win", "m_ones", "io_j", "io_g", "io_a", "af0", "af1", "io_r", "r0", "r1", "r2",
+              "vv", "a1", "a2", "a3", "cvt", "scat", "mm1", "cp1", "mm2", "b1", "b2", "gv", "gs", "c1", "c2", "c3",
+              "c4", "oc", "arr1", "arr2", "fg", "fin", "sent"]
 
 
 def _engines(mask):
     return [e for e in range(mask.bit_length()) if (mask >> e) & 1]
 
 
-def _hops(topo, a, b):
-    ca, cb = topo.chip(a), topo.chip(b)
-    if ca == cb:
-        return 0
-    if topo.mates(ca, cb) or topo.same_plane(ca, cb):
-        return 1
-    return 2
-
-
-def _all_to_all(g, core, T, topo, src, dst, remote_sem, local_sem):
-    me = T.rank_of(core)
-    peers = sorted([c for c in T.cores if c != core], key=lambda c: -_hops(topo, core, c))
-    width = min(len(_engines(topo.mask(core, c))) for c in peers)
-    n = 0
-    for i in range(0, len(peers), width):
-        used, trs = [], []
-        for c in peers[i:i + width]:
-            e = [k for k in _engines(topo.mask(core, c)) if k not in used][0]
-            used.append(e)
-            rid, pid, _ = topo.addr(c)
-            trs.append(RemoteDMATransfer(dst_ids=[DstId(rid=rid, pnc=pid)], dma_engine_mask=1 << e,
-                                         remote_sem=remote_sem, src=src[T.rank_of(c)], dst=dst[me]))
-            n += 1
-        g.remote_dma_fused(trs, local_sem=local_sem)
-    return n
+def _mask(engines):
+    return sum(1 << e for e in engines)
 
 
 def rank_program(g, core, T, topo):
@@ -66,75 +55,132 @@ def rank_program(g, core, T, topo):
     if r is None:
         return
     S = T.sem
+    A = AluOpType
     v, sc, sy, te = g.vector, g.scalar, g.sync, g.tensor
 
-    sy.dma_start(T.xs[:], T.x[:]).then_inc(S.xl, 16)
-    sy.dma_start(T.mid[r], T.x[R * r:R * r + R, :]).then_inc(S.own1, 16)
+    def near(a, b):
+        return topo.chip(a) == topo.chip(b) or topo.mates(topo.chip(a), topo.chip(b))
+    group = [c for c in T.cores if near(core, c)]
+    G = len(group)
+    base = T.rank_of(group[0])
+    P, l = base // G, r - base
+    lo, hi = C * l, C * l + C
+
+    sy.dma_start(T.xg[:, lo:hi], T.x[:]).then_inc(S.xl, 16)
     for k in range(8):
         sc.dma_start(T.g8i[16 * k:16 * k + 16, :], T.goes[:, 8 * k:8 * k + 8]).then_inc(S.gl, 16)
 
-    v.memset(T.ones[:], 1.0).then_inc(S.m_ones, 1)
+    v.memset(T.one8[:], 1.0).then_inc(S.m_o8, 1)
     v.memset(T.win[:], 0.0).then_inc(S.m_win, 1)
-    v.memset(T.off[:], 0).then_inc(S.m_off, 1)
-    v.memset(T.wdat[:], 0.0).then_inc(S.m_w, 1)
-    g.iota(T.vals[:], [[1, 128]], 0, 8, allow_small_or_imprecise_dtypes=True).then_inc(S.io_v, 1)
-    g.wait_ge(S.m_ones, 1)
-    g.affine_select(T.lead[:], T.ones[:, 0:8], [[-16, 8]], AluOpType.is_equal, 0.0, 0, 1).then_inc(S.io_e, 1)
-    g.affine_select(T.ident[:], T.ones[:], [[-1, 128]], AluOpType.is_equal, 0.0, 0, 1).then_inc(S.io_i, 1)
+    v.memset(T.ones[:], 1.0).then_inc(S.m_ones, 1)
+    g.iota(T.jm1[:], [[1, 128]], -1, 0, allow_small_or_imprecise_dtypes=True).then_inc(S.io_j, 1)
+    g.iota(T.gw[:], [[128, 8]], 0, 0, allow_small_or_imprecise_dtypes=True).then_inc(S.io_g, 1)
+    g.iota(T.pa[:], [[128, 4]], 0, 1).then_inc(S.io_a, 1)
+    g.wait_ge(S.m_o8, 1)
+    g.affine_select(T.comb[:, 0:8], T.one8[:], [[-16, 8]], A.is_equal, 0.0, 0, 1).then_inc(S.af0, 1)
+    g.wait_ge(S.io_g, 1)
+    g.affine_select(T.comb[:, 8:16], T.gw[:], [[-16, 8]], A.is_equal, 0.0, -1, 1).then_inc(S.af1, 1)
 
     g.wait_ge(S.xl, 16)
-    sent = _all_to_all(g, core, T, topo, T.xs, T.mid, S.arr1, S.sent)
+    far = [c for c in group if topo.chip(c) != topo.chip(core)]
+    off_e = _engines(topo.mask(core, far[0]))
+    share = len(off_e) // len(far)
+    trs, sent, arr1 = [], 0, 0
+    for c in group:
+        if c == core:
+            continue
+        if c in far:
+            i = far.index(c)
+            eng = off_e[share * i:share * i + share]
+        else:
+            eng = [e for e in _engines(topo.mask(core, c)) if e not in off_e]
+        rid, pid, _ = topo.addr(c)
+        trs.append(RemoteDMATransfer(dst_ids=[DstId(rid=rid, pnc=pid)], dma_engine_mask=_mask(eng),
+                                     remote_sem=S.arr1, src=T.xg[:, lo:hi], dst=T.xg[:, lo:hi]))
+        sent += len(eng)
+        arr1 += len(eng)
+    g.remote_dma_fused(trs, local_sem=S.sent)
 
-    v.wait_ge(S.io_e, 1)
-    v.tensor_reduce(T.sel[:, 0:1], T.lead[:, 0:8], AxisListType.X, AluOpType.add).then_inc(S.selr, 1)
+    g.wait_ge(S.m_ones, 1)
+    g.affine_select(T.rep[:], T.ones[:], [[-16, 4], [0, 8], [-1, 16]], A.is_equal, 0.0, -64 * (l % 2),
+                    1).then_inc(S.io_r, 1)
+
+    v.wait_ge(S.af0, 1)
+    v.tensor_reduce(T.sel0[:, 0:1], T.comb[:, 0:8], AxisListType.X, A.add).then_inc(S.r0, 1)
+    v.wait_ge(S.af1, 1)
+    v.tensor_reduce(T.rhsf[:, 0:1], T.comb[:, 0:16], AxisListType.X, A.add).then_inc(S.r1, 1)
+    v.wait_ge(S.r1, 1)
+    v.tensor_copy(T.rhsb[:], T.rhsf[:]).then_inc(S.r2, 1)
+    v.wait_ge(S.r0, 1)
+    v.wait_ge(S.io_j, 1)
+    v.tensor_scalar(T.vals[:], T.jm1[:], T.sel0[:, 0:1], 1.0, A.mult, A.add).then_inc(S.vv, 1)
+    v.wait_ge(S.io_a, 1)
+    v.tensor_scalar(T.j1[:], T.pa[:], 15, None, A.bitwise_and).then_inc(S.a1, 1)
+    v.tensor_scalar(T.j2[:], T.pa[:], 3, 48, A.logical_shift_right, A.bitwise_and).then_inc(S.a2, 1)
+    v.wait_ge(S.a1, 1)
+    v.wait_ge(S.a2, 1)
+    v.tensor_tensor(T.jj[:], T.j1[:], T.j2[:], A.add).then_inc(S.a3, 1)
     v.wait_ge(S.gl, 16 * 8)
     v.tensor_copy(T.g8u[:], T.g8i[:]).then_inc(S.cvt, 1)
     v.wait_ge(S.cvt, 1)
-    v.wait_ge(S.io_v, 1)
+    v.wait_ge(S.vv, 1)
     v.wait_ge(S.m_win, 1)
     v.tensor_copy(T.win[:, 0:NC].indirect(T.g8u[:, 0:8]), T.vals[:, 0:128]).then_inc(S.scat, 1)
     te.wait_ge(S.scat, 1)
-    te.wait_ge(S.selr, 1)
+    te.wait_ge(S.r2, 1)
     for k in range(8):
-        te.matmul(T.ps1[:, k:k + 1], T.win[:, 128 * k:128 * k + 128], T.sel[:, 0:1], True, True).then_inc(S.mm1, 1)
+        te.matmul(T.ps1[:, k:k + 1], T.win[:, 128 * k:128 * k + 128], T.rhsb[:, 0:1], True, True).then_inc(S.mm1, 1)
     v.wait_ge(S.mm1, 8)
     v.tensor_copy(T.invp[:], T.ps1[:, 0:8]).then_inc(S.cp1, 1)
     te.wait_ge(S.cp1, 1)
-    te.wait_ge(S.io_i, 1)
-    for a in range(8):
-        te.matmul(T.ps2[0:16, a:C:8], T.ident[:, 16 * a:16 * a + 16], T.invp[:, 0:8], True, True).then_inc(S.mm2, 1)
-    v.wait_ge(S.mm2, 8)
-    v.wait_ge(S.m_off, 1)
-    v.tensor_copy(T.off[0:16, :], T.ps2[0:16, 0:C]).then_inc(S.offr, 1)
+    te.wait_ge(S.io_r, 1)
+    for c in range(4):
+        te.matmul(T.ps2[:, c:16:4], T.rep[:, 128 * c:128 * c + 128], T.invp[:, l // 2:8:2], True,
+                  True).then_inc(S.mm2, 1)
+    v.wait_ge(S.mm2, 4)
+    v.tensor_scalar(T.t1[:], T.ps2[:, 0:16], float(-256 * P), 0.0, A.add, A.max).then_inc(S.b1, 1)
+    v.wait_ge(S.b1, 1)
+    v.tensor_scalar(T.l2[:], T.t1[:], 255.0, None, A.min).then_inc(S.b2, 1)
 
-    for q_, qs in ((sy, range(0, R, 2)), (sc, range(1, R, 2))):
-        q_.wait_ge(S.arr1, N - 1)
-        q_.wait_ge(S.own1, 16)
-        q_.wait_ge(S.m_w, 1)
-        for q in qs:
-            q_.dma_start(T.wdat[q:q + 1, :], T.mid[:, 16 * q:16 * q + 16, :]).then_inc(S.ld2, 16)
-
-    h = NC // 2
-    v.wait_ge(S.offr, 1)
-    v.wait_ge(S.ld2, 16 * R)
-    v.tensor_copy(T.ydat[:, 0:h], T.wdat[:, 0:NC].indirect(T.off[:, 0:C // 2])).then_inc(S.gv, 1)
-    sc.wait_ge(S.offr, 1)
-    sc.wait_ge(S.ld2, 16 * R)
-    sc.activation(T.ydat[:, h:NC], T.wdat[:, 0:NC].indirect(T.off[:, C // 2:C]),
+    v.wait_ge(S.b2, 1)
+    v.wait_ge(S.xl, 16)
+    v.wait_ge(S.arr1, arr1)
+    v.tensor_copy(T.sm[:, 0:128], T.xg[:, 0:256].indirect(T.l2[:, 0:8])).then_inc(S.gv, 1)
+    sc.wait_ge(S.b2, 1)
+    sc.wait_ge(S.xl, 16)
+    sc.wait_ge(S.arr1, arr1)
+    sc.activation(T.sm[:, 128:256], T.xg[:, 0:256].indirect(T.l2[:, 8:16]),
                   ActivationFunctionType.Copy).then_inc(S.gs, 1)
 
-    for q_, qs in ((sy, range(0, R, 2)), (sc, range(1, R, 2))):
-        q_.wait_ge(S.gv, 1)
-        q_.wait_ge(S.gs, 1)
-        for q in qs:
-            q_.dma_start(T.snd[:, 16 * q:16 * q + 16, :], T.ydat[q:q + 1, :]).then_inc(S.st2, 16)
-    sy.dma_start(T.ybuf[r], T.ydat[0:R, C * r:C * r + C]).then_inc(S.own2, 16)
+    g.wait_ge(S.gv, 1)
+    g.wait_ge(S.gs, 1)
+    arr2 = 0
+    for d in range(1, N // G):
+        Q = (P + d) % (N // G)
+        c = T.cores[G * Q + l]
+        m = topo.mask(core, c)
+        rid, pid, _ = topo.addr(c)
+        g.remote_dma(T.z[:, C * P:C * P + C], T.sm[:, C * Q:C * Q + C], S.arr2, S.sent, pid, rid, m)
+        sent += len(_engines(m))
+        arr2 += len(_engines(m))
 
-    g.wait_ge(S.st2, 16 * R)
-    sent += _all_to_all(g, core, T, topo, T.snd, T.ybuf, S.arr2, S.sent)
+    v.wait_ge(S.gv, 1)
+    v.wait_ge(S.gs, 1)
+    v.tensor_copy(T.z[:, C * P:C * P + C], T.sm[:, C * P:C * P + C]).then_inc(S.oc, 1)
+    v.tensor_copy(T.ii[:], T.ps2[:, 4 * P:4 * P + 4]).then_inc(S.c1, 1)
+    v.wait_ge(S.c1, 1)
+    v.tensor_scalar(T.p64[:], T.ii[:], 768, 2, A.bitwise_and, A.logical_shift_right).then_inc(S.c2, 1)
+    v.wait_ge(S.c2, 1)
+    v.wait_ge(S.a3, 1)
+    v.tensor_tensor(T.lfi[:], T.p64[:], T.jj[:], A.add).then_inc(S.c3, 1)
+    v.wait_ge(S.c3, 1)
+    v.tensor_copy(T.lf[:], T.lfi[:]).then_inc(S.c4, 1)
+    v.wait_ge(S.c4, 1)
+    v.wait_ge(S.oc, 1)
+    v.wait_ge(S.arr2, arr2)
+    v.tensor_copy(T.yo[:], T.z[:, 0:256].indirect(T.lf[:, 0:4])).then_inc(S.fg, 1)
 
-    sy.wait_ge(S.arr2, N - 1)
-    sy.wait_ge(S.own2, 16)
-    sy.dma_start(T.y[:], T.ybuf[:]).then_inc(S.fin, 16)
+    sy.wait_ge(S.fg, 1)
+    sy.dma_start(T.y[:], T.yo[:]).then_inc(S.fin, 16)
     sy.wait_ge(S.fin, 16)
     g.wait_ge(S.sent, sent)

@@ -15,31 +15,33 @@ SCRATCH = {
     "jm1": ("sbuf", [128, 128], "float32"),
     "gw": ("sbuf", [128, 8], "float32"),
     "one8": ("sbuf", [128, 8], "float32"),
-    "ones": ("sbuf", [128, 512], "float32"),
+    "ones": ("sbuf", [128, 128], "bfloat16"),
     "comb": ("sbuf", [128, 16], "float32"),
     "sel0": ("sbuf", [128, 1], "float32"),
     "rhsf": ("sbuf", [128, 1], "float32"),
     "rhsb": ("sbuf", [128, 1], "bfloat16"),
-    "rep": ("sbuf", [128, 512], "float32"),
+    "rept": ("sbuf", [128, 128], "bfloat16"),
     "g8i": ("sbuf", [128, 8], "int32"),
     "g8u": ("sbuf", [128, 8], "uint16"),
-    "invp": ("sbuf", [128, 8], "float32"),
     "t1": ("sbuf", [128, 16], "float32"),
-    "l2": ("sbuf", [128, 16], "uint16"),
+    "eb": ("sbuf", [128, 16], "bfloat16"),
     "ii": ("sbuf", [128, 4], "int32"),
+    "p64": ("sbuf", [128, 4], "int32"),
+    "p64b": ("sbuf", [128, 4], "bfloat16"),
+    "l2": ("sbuf", [128, 16], "uint16"),
     "pa": ("sbuf", [128, 4], "int32"),
     "j1": ("sbuf", [128, 4], "int32"),
     "j2": ("sbuf", [128, 4], "int32"),
-    "jj": ("sbuf", [128, 4], "int32"),
-    "p64": ("sbuf", [128, 4], "int32"),
-    "lfi": ("sbuf", [128, 4], "int32"),
+    "jj": ("sbuf", [128, 4], "float32"),
+    "lff": ("sbuf", [128, 4], "float32"),
     "lf": ("sbuf", [128, 4], "uint16"),
     "ps1": ("psum", [128, 512], "float32"),
     "ps2": ("psum", [128, 512], "float32"),
+    "ps3": ("psum", [128, 512], "float32"),
 }
 SEMAPHORES = ["xl", "gl", "m_o8", "m_win", "m_ones", "io_j", "io_g", "io_a", "af0", "af1", "io_r", "r0", "r1", "r2",
-              "vv", "a1", "a2", "a3", "cvt", "scat", "mm1", "cp1", "mm2", "b1", "b2", "gv", "gs", "c1", "c2", "c3",
-              "c4", "oc", "arr1", "arr2", "fg", "fin", "sent"]
+              "vv", "a1", "a2", "a3", "cvt", "scat", "mm1", "mm2", "mm3", "b1", "b2", "b3", "gv0", "gv1", "gv2", "gv3",
+              "gs0", "gs1", "gs2", "gs3", "c1", "c2", "c3", "c4", "c5", "arr1", "arr2", "fg", "fin", "sent"]
 
 
 def _engines(mask):
@@ -62,20 +64,20 @@ def rank_program(g, core, T, topo):
         return topo.chip(a) == topo.chip(b) or topo.mates(topo.chip(a), topo.chip(b))
     group = [c for c in T.cores if near(core, c)]
     G = len(group)
+    NG = N // G
     base = T.rank_of(group[0])
     P, l = base // G, r - base
     lo, hi = C * l, C * l + C
 
     sy.dma_start(T.xg[:, lo:hi], T.x[:]).then_inc(S.xl, 16)
     for k in range(8):
-        sc.dma_start(T.g8i[16 * k:16 * k + 16, :], T.goes[:, 8 * k:8 * k + 8]).then_inc(S.gl, 16)
+        (sc, sy)[k % 2].dma_start(T.g8i[16 * k:16 * k + 16, :], T.goes[:, 8 * k:8 * k + 8]).then_inc(S.gl, 16)
 
     v.memset(T.one8[:], 1.0).then_inc(S.m_o8, 1)
     v.memset(T.win[:], 0.0).then_inc(S.m_win, 1)
     v.memset(T.ones[:], 1.0).then_inc(S.m_ones, 1)
     g.iota(T.jm1[:], [[1, 128]], -1, 0, allow_small_or_imprecise_dtypes=True).then_inc(S.io_j, 1)
     g.iota(T.gw[:], [[128, 8]], 0, 0, allow_small_or_imprecise_dtypes=True).then_inc(S.io_g, 1)
-    g.iota(T.pa[:], [[128, 4]], 0, 1).then_inc(S.io_a, 1)
     g.wait_ge(S.m_o8, 1)
     g.affine_select(T.comb[:, 0:8], T.one8[:], [[-16, 8]], A.is_equal, 0.0, 0, 1).then_inc(S.af0, 1)
     g.wait_ge(S.io_g, 1)
@@ -85,25 +87,25 @@ def rank_program(g, core, T, topo):
     far = [c for c in group if topo.chip(c) != topo.chip(core)]
     off_e = _engines(topo.mask(core, far[0]))
     share = len(off_e) // len(far)
-    trs, sent, arr1 = [], 0, 0
-    for c in group:
-        if c == core:
-            continue
-        if c in far:
-            i = far.index(c)
-            eng = off_e[share * i:share * i + share]
-        else:
-            eng = [e for e in _engines(topo.mask(core, c)) if e not in off_e]
-        rid, pid, _ = topo.addr(c)
-        trs.append(RemoteDMATransfer(dst_ids=[DstId(rid=rid, pnc=pid)], dma_engine_mask=_mask(eng),
-                                     remote_sem=S.arr1, src=T.xg[:, lo:hi], dst=T.xg[:, lo:hi]))
-        sent += len(eng)
-        arr1 += len(eng)
-    g.remote_dma_fused(trs, local_sem=S.sent)
+    sent, arr1 = 0, 0
+    for batch in (far, [c for c in group if c != core and c not in far]):
+        trs = []
+        for c in batch:
+            if c in far:
+                i = far.index(c)
+                eng = off_e[share * i:share * i + share]
+            else:
+                eng = [e for e in _engines(topo.mask(core, c)) if e not in off_e][:share]
+            rid, pid, _ = topo.addr(c)
+            trs.append(RemoteDMATransfer(dst_ids=[DstId(rid=rid, pnc=pid)], dma_engine_mask=_mask(eng),
+                                         remote_sem=S.arr1, src=T.xg[:, lo:hi], dst=T.xg[:, lo:hi]))
+            sent += len(eng)
+            arr1 += len(eng)
+        g.remote_dma_fused(trs, local_sem=S.sent)
 
     g.wait_ge(S.m_ones, 1)
-    g.affine_select(T.rep[:], T.ones[:], [[-16, 4], [0, 8], [-1, 16]], A.is_equal, 0.0, -64 * (l % 2),
-                    1).then_inc(S.io_r, 1)
+    g.affine_select(T.rept[0:16, :], T.ones[0:16, :], [[0, 8], [-1, 16]], A.is_equal, 0.0, 0, 1).then_inc(S.io_r, 1)
+    g.iota(T.pa[:], [[128, 4]], 0, 1).then_inc(S.io_a, 1)
 
     v.wait_ge(S.af0, 1)
     v.tensor_reduce(T.sel0[:, 0:1], T.comb[:, 0:8], AxisListType.X, A.add).then_inc(S.r0, 1)
@@ -114,12 +116,6 @@ def rank_program(g, core, T, topo):
     v.wait_ge(S.r0, 1)
     v.wait_ge(S.io_j, 1)
     v.tensor_scalar(T.vals[:], T.jm1[:], T.sel0[:, 0:1], 1.0, A.mult, A.add).then_inc(S.vv, 1)
-    v.wait_ge(S.io_a, 1)
-    v.tensor_scalar(T.j1[:], T.pa[:], 15, None, A.bitwise_and).then_inc(S.a1, 1)
-    v.tensor_scalar(T.j2[:], T.pa[:], 3, 48, A.logical_shift_right, A.bitwise_and).then_inc(S.a2, 1)
-    v.wait_ge(S.a1, 1)
-    v.wait_ge(S.a2, 1)
-    v.tensor_tensor(T.jj[:], T.j1[:], T.j2[:], A.add).then_inc(S.a3, 1)
     v.wait_ge(S.gl, 16 * 8)
     v.tensor_copy(T.g8u[:], T.g8i[:]).then_inc(S.cvt, 1)
     v.wait_ge(S.cvt, 1)
@@ -128,55 +124,65 @@ def rank_program(g, core, T, topo):
     v.tensor_copy(T.win[:, 0:NC].indirect(T.g8u[:, 0:8]), T.vals[:, 0:128]).then_inc(S.scat, 1)
     te.wait_ge(S.scat, 1)
     te.wait_ge(S.r2, 1)
-    for k in range(8):
-        te.matmul(T.ps1[:, k:k + 1], T.win[:, 128 * k:128 * k + 128], T.rhsb[:, 0:1], True, True).then_inc(S.mm1, 1)
-    v.wait_ge(S.mm1, 8)
-    v.tensor_copy(T.invp[:], T.ps1[:, 0:8]).then_inc(S.cp1, 1)
-    te.wait_ge(S.cp1, 1)
-    te.wait_ge(S.io_r, 1)
-    for c in range(4):
-        te.matmul(T.ps2[:, c:16:4], T.rep[:, 128 * c:128 * c + 128], T.invp[:, l // 2:8:2], True,
-                  True).then_inc(S.mm2, 1)
-    v.wait_ge(S.mm2, 4)
-    v.tensor_scalar(T.t1[:], T.ps2[:, 0:16], float(-256 * P), 0.0, A.add, A.max).then_inc(S.b1, 1)
+    for n in range(4 * NG):
+        w0 = C * (G * (n // 4) + l) + 16 * (n % 4)
+        te.matmul(T.ps1[0:16, n:n + 1], T.win[:, w0:w0 + 16], T.rhsb[:, 0:1], True, True).then_inc(S.mm1, 1)
+    v.wait_ge(S.mm1, 4 * NG)
+    v.tensor_scalar(T.t1[0:16, :], T.ps1[0:16, 0:16], float(-256 * P), 0.0, A.add, A.max).then_inc(S.b1, 1)
     v.wait_ge(S.b1, 1)
-    v.tensor_scalar(T.l2[:], T.t1[:], 255.0, None, A.min).then_inc(S.b2, 1)
+    v.tensor_scalar(T.eb[0:16, :], T.t1[0:16, :], 255.0, None, A.min).then_inc(S.b2, 1)
+    te.wait_ge(S.b2, 1)
+    te.wait_ge(S.io_r, 1)
+    te.matmul(T.ps2[:, 0:16], T.rept[0:16, :], T.eb[0:16, :], True, True).then_inc(S.mm2, 1)
+    v.wait_ge(S.mm2, 1)
+    v.tensor_copy(T.l2[:], T.ps2[:, 0:16]).then_inc(S.b3, 1)
 
-    v.wait_ge(S.b2, 1)
-    v.wait_ge(S.xl, 16)
-    v.wait_ge(S.arr1, arr1)
-    v.tensor_copy(T.sm[:, 0:128], T.xg[:, 0:256].indirect(T.l2[:, 0:8])).then_inc(S.gv, 1)
-    sc.wait_ge(S.b2, 1)
-    sc.wait_ge(S.xl, 16)
-    sc.wait_ge(S.arr1, arr1)
-    sc.activation(T.sm[:, 128:256], T.xg[:, 0:256].indirect(T.l2[:, 8:16]),
-                  ActivationFunctionType.Copy).then_inc(S.gs, 1)
+    for q_ in (v, sc):
+        q_.wait_ge(S.b3, 1)
+        q_.wait_ge(S.xl, 16)
+        q_.wait_ge(S.arr1, arr1)
+    h = C // 2
+    for d in (1, 2, 3, 0):
+        Q = (P + d) % NG
+        out = T.z if d == 0 else T.sm
+        v.tensor_copy(out[:, C * Q:C * Q + h],
+                      T.xg[:, 0:256].indirect(T.l2[:, 4 * Q:4 * Q + 2])).then_inc(S["gv%d" % d], 1)
+        sc.activation(out[:, C * Q + h:C * Q + C], T.xg[:, 0:256].indirect(T.l2[:, 4 * Q + 2:4 * Q + 4]),
+                      ActivationFunctionType.Copy).then_inc(S["gs%d" % d], 1)
 
-    g.wait_ge(S.gv, 1)
-    g.wait_ge(S.gs, 1)
     arr2 = 0
-    for d in range(1, N // G):
-        Q = (P + d) % (N // G)
+    for d in (1, 2, 3):
+        Q = (P + d) % NG
         c = T.cores[G * Q + l]
         m = topo.mask(core, c)
         rid, pid, _ = topo.addr(c)
+        g.wait_ge(S["gv%d" % d], 1)
+        g.wait_ge(S["gs%d" % d], 1)
         g.remote_dma(T.z[:, C * P:C * P + C], T.sm[:, C * Q:C * Q + C], S.arr2, S.sent, pid, rid, m)
         sent += len(_engines(m))
         arr2 += len(_engines(m))
 
-    v.wait_ge(S.gv, 1)
-    v.wait_ge(S.gs, 1)
-    v.tensor_copy(T.z[:, C * P:C * P + C], T.sm[:, C * P:C * P + C]).then_inc(S.oc, 1)
-    v.tensor_copy(T.ii[:], T.ps2[:, 4 * P:4 * P + 4]).then_inc(S.c1, 1)
+    v.wait_ge(S.io_a, 1)
+    v.tensor_scalar(T.j1[:], T.pa[:], 15, None, A.bitwise_and).then_inc(S.a1, 1)
+    v.tensor_scalar(T.j2[:], T.pa[:], 3, 48, A.logical_shift_right, A.bitwise_and).then_inc(S.a2, 1)
+    v.tensor_copy(T.ii[0:16, :], T.ps1[0:16, 4 * P:4 * P + 4]).then_inc(S.c1, 1)
+    v.wait_ge(S.a1, 1)
+    v.wait_ge(S.a2, 1)
+    v.tensor_tensor(T.jj[:], T.j1[:], T.j2[:], A.add).then_inc(S.a3, 1)
     v.wait_ge(S.c1, 1)
-    v.tensor_scalar(T.p64[:], T.ii[:], 768, 2, A.bitwise_and, A.logical_shift_right).then_inc(S.c2, 1)
+    v.tensor_scalar(T.p64[0:16, :], T.ii[0:16, :], 768, 2, A.bitwise_and, A.logical_shift_right).then_inc(S.c2, 1)
     v.wait_ge(S.c2, 1)
+    v.tensor_copy(T.p64b[0:16, :], T.p64[0:16, :]).then_inc(S.c3, 1)
+    te.wait_ge(S.c3, 1)
+    te.matmul(T.ps3[:, 0:4], T.rept[0:16, :], T.p64b[0:16, :], True, True).then_inc(S.mm3, 1)
+    v.wait_ge(S.mm3, 1)
     v.wait_ge(S.a3, 1)
-    v.tensor_tensor(T.lfi[:], T.p64[:], T.jj[:], A.add).then_inc(S.c3, 1)
-    v.wait_ge(S.c3, 1)
-    v.tensor_copy(T.lf[:], T.lfi[:]).then_inc(S.c4, 1)
+    v.tensor_tensor(T.lff[:], T.ps3[:, 0:4], T.jj[:], A.add).then_inc(S.c4, 1)
     v.wait_ge(S.c4, 1)
-    v.wait_ge(S.oc, 1)
+    v.tensor_copy(T.lf[:], T.lff[:]).then_inc(S.c5, 1)
+    v.wait_ge(S.c5, 1)
+    v.wait_ge(S.gv0, 1)
+    v.wait_ge(S.gs0, 1)
     v.wait_ge(S.arr2, arr2)
     v.tensor_copy(T.yo[:], T.z[:, 0:256].indirect(T.lf[:, 0:4])).then_inc(S.fg, 1)
 

from concourse.bass import DstId, RemoteDMATransfer
from concourse.mybir import AluOpType, AxisListType, ActivationFunctionType

N = 16
C = 64
NC = N * C

SCRATCH = {
    "xg": ("sbuf", [128, 256], "float32"),
    "sm": ("sbuf", [128, 256], "float32"),
    "z": ("sbuf", [128, 256], "float32"),
    "yo": ("sbuf", [128, C], "float32"),
    "win": ("sbuf", [128, NC], "bfloat16"),
    "vals": ("sbuf", [128, 128], "bfloat16"),
    "jm1": ("sbuf", [128, 128], "float32"),
    "gw": ("sbuf", [128, 8], "float32"),
    "one8": ("sbuf", [128, 8], "float32"),
    "ones": ("sbuf", [128, 128], "bfloat16"),
    "comb": ("sbuf", [128, 16], "float32"),
    "sel0": ("sbuf", [128, 1], "float32"),
    "rhsf": ("sbuf", [128, 1], "float32"),
    "rhsb": ("sbuf", [128, 1], "bfloat16"),
    "rept": ("sbuf", [128, 128], "bfloat16"),
    "g8i": ("sbuf", [128, 8], "int32"),
    "g8u": ("sbuf", [128, 8], "uint16"),
    "t1": ("sbuf", [128, 16], "float32"),
    "eb": ("sbuf", [128, 16], "bfloat16"),
    "ii": ("sbuf", [128, 4], "int32"),
    "p64": ("sbuf", [128, 4], "int32"),
    "p64b": ("sbuf", [128, 4], "bfloat16"),
    "l2": ("sbuf", [128, 16], "uint16"),
    "pa": ("sbuf", [128, 4], "int32"),
    "j1": ("sbuf", [128, 4], "int32"),
    "j2": ("sbuf", [128, 4], "int32"),
    "jj": ("sbuf", [128, 4], "float32"),
    "lff": ("sbuf", [128, 4], "float32"),
    "lf": ("sbuf", [128, 4], "uint16"),
    "ps1": ("psum", [128, 512], "float32"),
    "ps2": ("psum", [128, 512], "float32"),
    "ps3": ("psum", [128, 512], "float32"),
}
SEMAPHORES = ["xl", "gl", "m_o8", "m_win", "m_ones", "io_j", "io_g", "io_a", "af0", "af1", "io_r", "r0", "r1", "r2",
              "vv", "a1", "a2", "a3", "cvt", "scat", "mm1", "mm2", "mm3", "b1", "b2", "b3", "gv0", "gv1", "gv2", "gv3",
              "gs0", "gs1", "gs2", "gs3", "c1", "c2", "c3", "c4", "c5", "arr1", "arr2", "fg", "fin", "sent"]


def _engines(mask):
    return [e for e in range(mask.bit_length()) if (mask >> e) & 1]


def _mask(engines):
    return sum(1 << e for e in engines)


def rank_program(g, core, T, topo):
    r = T.rank_of(core)
    if r is None:
        return
    S = T.sem
    A = AluOpType
    v, sc, sy, te = g.vector, g.scalar, g.sync, g.tensor

    def near(a, b):
        return topo.chip(a) == topo.chip(b) or topo.mates(topo.chip(a), topo.chip(b))
    group = [c for c in T.cores if near(core, c)]
    G = len(group)
    NG = N // G
    base = T.rank_of(group[0])
    P, l = base // G, r - base
    lo, hi = C * l, C * l + C

    sy.dma_start(T.xg[:, lo:hi], T.x[:]).then_inc(S.xl, 16)
    for k in range(8):
        (sc, sy)[k % 2].dma_start(T.g8i[16 * k:16 * k + 16, :], T.goes[:, 8 * k:8 * k + 8]).then_inc(S.gl, 16)

    v.memset(T.one8[:], 1.0).then_inc(S.m_o8, 1)
    v.memset(T.win[:], 0.0).then_inc(S.m_win, 1)
    v.memset(T.ones[:], 1.0).then_inc(S.m_ones, 1)
    g.iota(T.jm1[:], [[1, 128]], -1, 0, allow_small_or_imprecise_dtypes=True).then_inc(S.io_j, 1)
    g.iota(T.gw[:], [[128, 8]], 0, 0, allow_small_or_imprecise_dtypes=True).then_inc(S.io_g, 1)
    g.wait_ge(S.m_o8, 1)
    g.affine_select(T.comb[:, 0:8], T.one8[:], [[-16, 8]], A.is_equal, 0.0, 0, 1).then_inc(S.af0, 1)
    g.wait_ge(S.io_g, 1)
    g.affine_select(T.comb[:, 8:16], T.gw[:], [[-16, 8]], A.is_equal, 0.0, -1, 1).then_inc(S.af1, 1)

    g.wait_ge(S.xl, 16)
    far = [c for c in group if topo.chip(c) != topo.chip(core)]
    off_e = _engines(topo.mask(core, far[0]))
    share = len(off_e) // len(far)
    sent, arr1 = 0, 0
    for batch in (far, [c for c in group if c != core and c not in far]):
        trs = []
        for c in batch:
            if c in far:
                i = far.index(c)
                eng = off_e[share * i:share * i + share]
            else:
                eng = [e for e in _engines(topo.mask(core, c)) if e not in off_e][:share]
            rid, pid, _ = topo.addr(c)
            trs.append(RemoteDMATransfer(dst_ids=[DstId(rid=rid, pnc=pid)], dma_engine_mask=_mask(eng),
                                         remote_sem=S.arr1, src=T.xg[:, lo:hi], dst=T.xg[:, lo:hi]))
            sent += len(eng)
            arr1 += len(eng)
        g.remote_dma_fused(trs, local_sem=S.sent)

    g.wait_ge(S.m_ones, 1)
    g.affine_select(T.rept[0:16, :], T.ones[0:16, :], [[0, 8], [-1, 16]], A.is_equal, 0.0, 0, 1).then_inc(S.io_r, 1)
    g.iota(T.pa[:], [[128, 4]], 0, 1).then_inc(S.io_a, 1)

    v.wait_ge(S.af0, 1)
    v.tensor_reduce(T.sel0[:, 0:1], T.comb[:, 0:8], AxisListType.X, A.add).then_inc(S.r0, 1)
    v.wait_ge(S.af1, 1)
    v.tensor_reduce(T.rhsf[:, 0:1], T.comb[:, 0:16], AxisListType.X, A.add).then_inc(S.r1, 1)
    v.wait_ge(S.r1, 1)
    v.tensor_copy(T.rhsb[:], T.rhsf[:]).then_inc(S.r2, 1)
    v.wait_ge(S.r0, 1)
    v.wait_ge(S.io_j, 1)
    v.tensor_scalar(T.vals[:], T.jm1[:], T.sel0[:, 0:1], 1.0, A.mult, A.add).then_inc(S.vv, 1)
    v.wait_ge(S.gl, 16 * 8)
    v.tensor_copy(T.g8u[:], T.g8i[:]).then_inc(S.cvt, 1)
    v.wait_ge(S.cvt, 1)
    v.wait_ge(S.vv, 1)
    v.wait_ge(S.m_win, 1)
    v.tensor_copy(T.win[:, 0:NC].indirect(T.g8u[:, 0:8]), T.vals[:, 0:128]).then_inc(S.scat, 1)
    te.wait_ge(S.scat, 1)
    te.wait_ge(S.r2, 1)
    for n in range(4 * NG):
        w0 = C * (G * (n // 4) + l) + 16 * (n % 4)
        te.matmul(T.ps1[0:16, n:n + 1], T.win[:, w0:w0 + 16], T.rhsb[:, 0:1], True, True).then_inc(S.mm1, 1)
    v.wait_ge(S.mm1, 4 * NG)
    v.tensor_scalar(T.t1[0:16, :], T.ps1[0:16, 0:16], float(-256 * P), 0.0, A.add, A.max).then_inc(S.b1, 1)
    v.wait_ge(S.b1, 1)
    v.tensor_scalar(T.eb[0:16, :], T.t1[0:16, :], 255.0, None, A.min).then_inc(S.b2, 1)
    te.wait_ge(S.b2, 1)
    te.wait_ge(S.io_r, 1)
    te.matmul(T.ps2[:, 0:16], T.rept[0:16, :], T.eb[0:16, :], True, True).then_inc(S.mm2, 1)
    v.wait_ge(S.mm2, 1)
    v.tensor_copy(T.l2[:], T.ps2[:, 0:16]).then_inc(S.b3, 1)

    for q_ in (v, sc):
        q_.wait_ge(S.b3, 1)
        q_.wait_ge(S.xl, 16)
        q_.wait_ge(S.arr1, arr1)
    h = C // 2
    for d in (1, 2, 3, 0):
        Q = (P + d) % NG
        out = T.z if d == 0 else T.sm
        v.tensor_copy(out[:, C * Q:C * Q + h],
                      T.xg[:, 0:256].indirect(T.l2[:, 4 * Q:4 * Q + 2])).then_inc(S["gv%d" % d], 1)
        sc.activation(out[:, C * Q + h:C * Q + C], T.xg[:, 0:256].indirect(T.l2[:, 4 * Q + 2:4 * Q + 4]),
                      ActivationFunctionType.Copy).then_inc(S["gs%d" % d], 1)

    arr2 = 0
    for d in (1, 2, 3):
        Q = (P + d) % NG
        c = T.cores[G * Q + l]
        m = topo.mask(core, c)
        rid, pid, _ = topo.addr(c)
        g.wait_ge(S["gv%d" % d], 1)
        g.wait_ge(S["gs%d" % d], 1)
        g.remote_dma(T.z[:, C * P:C * P + C], T.sm[:, C * Q:C * Q + C], S.arr2, S.sent, pid, rid, m)
        sent += len(_engines(m))
        arr2 += len(_engines(m))

    v.wait_ge(S.io_a, 1)
    v.tensor_scalar(T.j1[:], T.pa[:], 15, None, A.bitwise_and).then_inc(S.a1, 1)
    v.tensor_scalar(T.j2[:], T.pa[:], 3, 48, A.logical_shift_right, A.bitwise_and).then_inc(S.a2, 1)
    v.tensor_copy(T.ii[0:16, :], T.ps1[0:16, 4 * P:4 * P + 4]).then_inc(S.c1, 1)
    v.wait_ge(S.a1, 1)
    v.wait_ge(S.a2, 1)
    v.tensor_tensor(T.jj[:], T.j1[:], T.j2[:], A.add).then_inc(S.a3, 1)
    v.wait_ge(S.c1, 1)
    v.tensor_scalar(T.p64[0:16, :], T.ii[0:16, :], 768, 2, A.bitwise_and, A.logical_shift_right).then_inc(S.c2, 1)
    v.wait_ge(S.c2, 1)
    v.tensor_copy(T.p64b[0:16, :], T.p64[0:16, :]).then_inc(S.c3, 1)
    te.wait_ge(S.c3, 1)
    te.matmul(T.ps3[:, 0:4], T.rept[0:16, :], T.p64b[0:16, :], True, True).then_inc(S.mm3, 1)
    v.wait_ge(S.mm3, 1)
    v.wait_ge(S.a3, 1)
    v.tensor_tensor(T.lff[:], T.ps3[:, 0:4], T.jj[:], A.add).then_inc(S.c4, 1)
    v.wait_ge(S.c4, 1)
    v.tensor_copy(T.lf[:], T.lff[:]).then_inc(S.c5, 1)
    v.wait_ge(S.c5, 1)
    v.wait_ge(S.gv0, 1)
    v.wait_ge(S.gs0, 1)
    v.wait_ge(S.arr2, arr2)
    v.tensor_copy(T.yo[:], T.z[:, 0:256].indirect(T.lf[:, 0:4])).then_inc(S.fg, 1)

    sy.wait_ge(S.fg, 1)
    sy.dma_start(T.y[:], T.yo[:]).then_inc(S.fin, 16)
    sy.wait_ge(S.fin, 16)
    g.wait_ge(S.sent, sent)
